import numpy as np
import ml_dtypes


def mxq(x, axis, fmt="e4m3"):
    dtype, down = {"e4m3": (ml_dtypes.float8_e4m3fn, 7), "e5m2": (ml_dtypes.float8_e5m2, 14)}[fmt]
    v = np.moveaxis(np.asarray(x, np.float32).astype(ml_dtypes.bfloat16).astype(np.float64), axis, -1)
    blocks = v.reshape(v.shape[:-1] + (-1, 32))
    amax = np.abs(blocks).max(-1, keepdims=True)
    byte = np.maximum(np.where(amax > 0, np.frexp(amax)[1] - 1 + 127, 0) - down, 1)
    scale = np.exp2(byte - 127.0)
    codes = (blocks / scale).astype(np.float32).astype(dtype).astype(np.float64)
    return np.moveaxis((codes * scale).reshape(v.shape), -1, axis)


WIDE = False


def mx_kscale(k):
    if not WIDE:
        return np.ones(k)
    levels = np.array([10, -10, 5, -5, 0])
    if k % 512:
        return np.exp2(np.random.permutation(np.resize(levels, k // 32))).repeat(32)
    a = np.empty((k // 512, 16))
    for p in range(k // 512):
        a[p, :8] = np.random.permutation(np.resize(levels, 8))
        for g in range(8):
            far = levels[np.abs(levels - a[p, g]) >= 10]
            a[p, g + 8] = far[np.random.randint(len(far))]
    return np.exp2(a.ravel()).repeat(32)


def f64(x):
    return np.asarray(x).astype(np.float64)


def striped(idx):
    return np.tile(idx.reshape(-1, 16).T, (8, 1)).astype(np.uint16)


def unstriped(offs):
    return offs[:16].T.reshape(-1).astype(np.int64)


E2M1 = np.array([0.0, 0.5, 1.0, 1.5, 2.0, 3.0, 4.0, 6.0, -0.0, -0.5, -1.0, -1.5, -2.0, -3.0, -4.0, -6.0])


def pack_weight(w, fmt):
    k, n = w.shape
    w = f64(np.asarray(w, np.float32).astype(ml_dtypes.bfloat16)).reshape(k // 32, 32, n)
    amax = np.abs(w).max(1)
    if fmt == "e4m3":
        byte = np.frexp(amax)[1] - 1 + 127 - 7
    else:
        mant, ex = np.frexp(amax / 6.0)
        byte = np.where(mant > 0.5, ex, ex - 1) + 127
    byte = np.clip(np.where(amax > 0, byte, 1), 1, 254)
    scaled = (w * np.exp2(127.0 - byte)[:, None, :]).reshape(k, n).astype(np.float32)
    by_word = np.ascontiguousarray(scaled.reshape(k // 512, 128, 4, n).transpose(0, 1, 3, 2))
    if fmt == "e4m3":
        words = by_word.astype(ml_dtypes.float8_e4m3fn).view(np.uint8)
    else:
        c = by_word.astype(ml_dtypes.float4_e2m1fn).view(np.uint8) & 0xF
        words = (c[..., 0::2] | (c[..., 1::2] << 4)).reshape(k // 512, 128, 2 * n)
    return np.ascontiguousarray(words), np.ascontiguousarray(byte.astype(np.uint8).reshape(k // 512, 16, n))


def unpack_weight(words, scales, fmt):
    g, _, n = scales.shape
    words = np.ascontiguousarray(words).reshape(g, 128, n, -1)
    if fmt == "e4m3":
        vals = words.view(ml_dtypes.float8_e4m3fn).astype(np.float64)
    else:
        nib = np.empty((g, 128, n, 4), np.uint8)
        nib[..., 0::2] = words & 0xF
        nib[..., 1::2] = words >> 4
        vals = E2M1[nib]
    vals = vals * np.repeat(np.exp2(scales.astype(np.float64) - 127.0), 8, axis=1)[..., None]
    return vals.transpose(0, 1, 3, 2).reshape(g * 512, n)


def gelu(v):
    return 0.5 * v * (1.0 + np.tanh(np.sqrt(2.0 / np.pi) * (v + 0.044715 * v**3)))


K, T, S, H, N, T2, P = 1024, 2048, 1024, 1024, 384, 2048, 1024

def setup_inputs():
    n = np.random.standard_normal
    s = mx_kscale(K)[:, None]
    u = mx_kscale(H)[:, None]
    d = {}
    d["tab_words"], d["tab_scales"] = pack_weight(n((K, T)) * s, "e4m3")
    d["offs"] = striped(np.random.permutation(T)[:S])
    d["w1"] = (0.56 * n((K, H)) / K ** 0.5 / s).astype(np.float32)
    sign = np.random.choice([-1.0, 1.0], H)
    d["slope"] = (sign * np.random.uniform(1.5, 4.0, H)).astype(np.float32)
    d["gain"] = (np.random.uniform(-1.6, 1.6, H) * u[:, 0]).astype(np.float32)
    d["wgs"] = np.exp(0.3 * n((128, S))).astype(np.float32)
    d["page0"] = (0.8 * n((H, T2)) * u).astype(np.float32)
    d["offs2"] = striped(np.random.permutation(T2)[:S])
    d["offs3"] = striped(np.random.permutation(T2)[:P])
    d["w2"] = (0.9 * n((H, N)) / H ** 0.5 / u).astype(np.float32)
    d["w4_words"], d["w4_scales"] = pack_weight(0.9 * n((H, N)) / H ** 0.5 / u, "e2m1")
    d["page1"] = (0.6 * n((N, T2))).astype(np.float32)
    d["wgo"] = np.exp(0.3 * n((128, P))).astype(np.float32)
    d["offs4"] = striped(np.random.permutation(T2)[:P])
    return d

def reference(tab_words, tab_scales, offs, w1, slope, gain, wgs, page0, offs2, offs3, w2, w4_words, w4_scales, page1, wgo, offs4):
    v = unpack_weight(tab_words, tab_scales, "e4m3")[:, unstriped(offs)]
    e = mxq(f64(w1), 0, "e4m3").T @ v
    h = f64(gain)[:, None] * (np.tanh(f64(slope)[:, None] * e) + np.cos(e))
    page = f64(page0).copy()
    page[:, unstriped(offs2)] = np.tile(f64(wgs), (H // 128, 1)) * h
    x = page[:, unstriped(offs3)]
    xq = mxq(x, 0, "e4m3")
    xm = mxq(np.abs(x), 0, "e4m3")
    w4 = unpack_weight(w4_words, w4_scales, "e2m1")
    y = np.tanh(mxq(f64(w2), 0, "e4m3").T @ xq + w4.T @ xm)
    out = f64(page1).copy()
    out[:, unstriped(offs4)] = np.tile(f64(wgo), (N // 128, 1)) * y
    return out

@@ -1,0 +1,424 @@
+import math
+from contextlib import ExitStack
+
+import concourse.mybir as mybir
+
+K, T, S, H, N, T2 = 1024, 2048, 1024, 1024, 384, 2048
+FLOPS = 2 * K * H * S + 4 * H * N * S
+
+F32 = mybir.dt.float32
+BF16 = mybir.dt.bfloat16
+I32 = mybir.dt.int32
+U32 = mybir.dt.uint32
+U16 = mybir.dt.uint16
+U8 = mybir.dt.uint8
+FP8X4 = mybir.dt.float8_e4m3fn_x4
+FP4X4 = mybir.dt.float4_e2m1fn_x4
+ACT = mybir.ActivationFunctionType
+ALU = mybir.AluOpType
+
+P = 128
+PACK = 4
+KP = P * PACK
+HALF = 512
+PASSES = K // KP
+TILES = H // P
+NT = N // P
+TWO_PI = 2.0 * math.pi
+LOW, HIGH, WHOLE = slice(0, HALF), slice(HALF, S), slice(0, S)
+CHUNKS = (slice(0, 256), slice(256, 512), slice(512, 1024))
+
+
+def tile_list_cabinet_repair_page_kernel(
+    tc, tab_words, tab_scales, offs, w1, slope, gain, wgs, page0, offs2, offs3, w2, w4_words, w4_scales, page1, wgo, offs4, out
+):
+    nc = tc.nc
+    with ExitStack() as ctx:
+        lists = ctx.enter_context(tc.tile_pool(name="lists", bufs=1))
+        keep = ctx.enter_context(tc.tile_pool(name="keep", bufs=1))
+        ring = ctx.enter_context(tc.tile_pool(name="ring", bufs=2))
+        pages = ctx.enter_context(tc.tile_pool(name="pages", bufs=5))
+        psum = ctx.enter_context(tc.psum_pool(name="psum", bufs=4))
+
+        def load_list(src, name):
+            t = lists.tile([P, S // 16], U16, name=name)
+            nc.sync.dma_start(t[:], src)
+            return t
+
+        def entries(lst, c):
+            return lst[:, c.start // 16 : c.stop // 16]
+
+        tab_sc = keep.tile([P, T], U8, name="tab_sc", align_bytes=64)
+        nc.gpsimd.memset(tab_sc[:].bitcast(I32), 0)
+        for q in range(4):
+            nc.gpsimd.dma_start(
+                tab_sc[32 * q : 32 * q + 8, :].bitcast(I32), tab_scales[:, 4 * q : 4 * q + 4, :].bitcast(I32)
+            )
+        ones = keep.tile([P, 1], F32, name="ones")
+        nc.vector.memset(ones[:], 1.0)
+        zero_in = keep.tile([P, 1], F32, name="zero_in")
+        nc.vector.memset(zero_in[:], 0.0)
+        zero = keep.tile([P, 1], F32, name="zero")
+        nc.scalar.activation(zero[:], zero_in[:], ACT.Silu)
+        half_pi = keep.tile([P, 1], F32, name="half_pi")
+        nc.vector.tensor_scalar(half_pi[:], ones[:], math.pi / 2, None, ALU.mult)
+        w4s = keep.tile([P, PASSES, N], U8, name="w4s", align_bytes=64)
+        nc.vector.memset(w4s[:].bitcast(I32), 0)
+
+        def load_tab(a):
+            t = keep.tile([P, T], I32, name="big%d" % a, align_bytes=64)
+            nc.sync.dma_start(t[:], tab_words[a].rearrange("p t i -> p (t i)").bitcast(I32))
+            return t
+
+        def load_w1(b, a):
+            if (b, a) == (0, 0):
+                raw = keep.tile([P, PACK, KP], F32, name="wgs1")
+            else:
+                raw = ring.tile([P, PACK, KP], F32, name="raw", align_bytes=64)
+            src = w1[a * KP : (a + 1) * KP, b * KP : (b + 1) * KP].rearrange("(p i) r -> p i r", i=PACK)
+            nc.sync.dma_start(raw[:], src)
+            return raw
+
+        def cast_w1(raw, on_vector):
+            if on_vector:
+                wb = keep.tile([P, PACK * KP], BF16, name="late_words", align_bytes=64)
+            else:
+                wb = ring.tile([P, PACK * KP], BF16, name="xa", align_bytes=64)
+            dst = wb[:].rearrange("p (t m i) -> p m i t", t=PACK, i=PACK)
+            src = raw[:].rearrange("p i (m t) -> p m i t", t=PACK)
+            if on_vector:
+                nc.vector.tensor_copy(dst, src)
+            else:
+                nc.scalar.copy(dst, src)
+            return wb
+
+        def quantize(src, name):
+            width = src.shape[1] // PACK
+            codes = keep.tile([P, width], U32, name=name + "_c", align_bytes=64)
+            scales = keep.tile([P, width], U8, name=name + "_s", align_bytes=64)
+            nc.vector.quantize_mx(out=codes[:].bitcast(FP8X4), scales=scales[:], in_=src)
+            return codes, scales
+
+        wgs_rows = wgs.rearrange("(q t) j -> q t j", t=PACK)
+        wgs_t = {}
+
+        def load_wgs(queue, t0, groups):
+            w = keep.tile([P, groups[-1][1] - t0, S], F32, name="wgs%d" % t0)
+            for lo, hi in groups:
+                for q in range(4):
+                    queue.dma_start(w[32 * q : 32 * q + 32, lo - t0 : hi - t0, :], wgs_rows[:, lo:hi, :])
+                for t in range(lo, hi):
+                    wgs_t[t] = w[:, t - t0, :]
+
+        page_rows = page0.rearrange("(b p t) m -> b t p m", p=P, t=PACK)
+        page = {}
+
+        def load_page(i):
+            page[i] = pages.tile([P, T2], F32, name="page")
+            nc.sync.dma_start(page[i][:], page_rows[i // PACK, i % PACK])
+
+        raws = {}
+        o1 = load_list(offs, "o1")
+        tab = [load_tab(0)]
+        raws[0, 0] = load_w1(0, 0)
+        tab.append(load_tab(1))
+        raws[0, 1] = load_w1(0, 1)
+        slope_t = keep.tile([P, PASSES, PACK], F32, name="slope_t")
+        nc.sync.dma_start(slope_t[:], slope.rearrange("(b p t) -> p b t", p=P, t=PACK))
+        gain_t = keep.tile([P, PASSES, PACK], F32, name="gain_t")
+        nc.sync.dma_start(gain_t[:], gain.rearrange("(b p t) -> p b t", p=P, t=PACK))
+        load_wgs(nc.sync, 0, [(0, 1)])
+        o2 = load_list(offs2, "o2")
+        load_page(0)
+        o3 = load_list(offs3, "o3")
+
+        vw, vs = {}, {}
+
+        def pick_words(a, c):
+            if c.start == 0:
+                vw[a, 0] = keep.tile([P, HALF], U32, name="vw%d" % a, align_bytes=64)
+            elif a == 0:
+                late = keep.tile([P, PASSES, HALF], U32, name="late_words", align_bytes=64)
+                for n in range(PASSES):
+                    vw[n, c.start] = late[:, n, :]
+            nc.vector.tensor_copy(vw[a, c.start][:], tab[a][:].bitcast(U32).indirect(entries(o1, c)))
+
+        def pick_scales(c):
+            vs[c.start] = keep.tile([P, HALF], U8, name="vs%d" % c.start, align_bytes=64)
+            nc.vector.tensor_copy(vs[c.start][:], tab_sc[:].indirect(entries(o1, c)))
+
+        w1q = {}
+        pick_words(0, LOW)
+        pick_scales(LOW)
+        wb00 = cast_w1(raws[0, 0], False)
+        pick_words(1, LOW)
+        w1q[0, 0] = quantize(wb00[:], "w1q00")
+        wb01 = cast_w1(raws[0, 1], True)
+        w1q[0, 1] = quantize(wb01[:], "w1q01")
+        pick_words(0, HIGH)
+        pick_scales(HIGH)
+        pick_words(1, HIGH)
+        load_wgs(nc.gpsimd, 1, [(1, 2), (2, 4)])
+        raws[1, 0] = load_w1(1, 0)
+        load_page(1)
+        raws[1, 1] = load_w1(1, 1)
+
+        mag, turns, th, gw, red, cs, bank = {}, {}, {}, {}, {}, {}, {}
+
+        def angle(i, c):
+            b, t = divmod(i, PACK)
+            e = psum.tile([P, HALF], F32, name="e")
+            for a in range(PASSES):
+                codes, scales = w1q[b, a]
+                nc.tensor.matmul_mx(
+                    out=e[:],
+                    lhsT=codes[:, t * P : (t + 1) * P].bitcast(FP8X4),
+                    lhsT_scale=scales[:, t * P : (t + 1) * P],
+                    rhs=vw[a, c.start][:].bitcast(FP8X4),
+                    rhs_scale=vs[c.start][4 * a : P, :],
+                    start=(a == 0),
+                    stop=(a == PASSES - 1),
+                )
+            if c.start == 0:
+                mag[i] = ring.tile([P, S], F32, name="mag", bufs=4)
+                turns[i] = ring.tile([P, S], F32, name="turns", bufs=3, align_bytes=64)
+                red[i] = ring.tile([P, S], F32, name="red", bufs=3)
+            nc.scalar.activation(mag[i][:, c], e[:], ACT.Abs)
+            nc.scalar.activation(turns[i][:, c].bitcast(U32), mag[i][:, c], ACT.Copy, bias=-0.25, scale=1.0 / TWO_PI)
+            bank[i, c.start] = e
+
+        def reduce_angle(i, c):
+            nc.vector.scalar_tensor_tensor(red[i][:, c], turns[i][:, c].bitcast(I32), -TWO_PI, mag[i][:, c], ALU.mult, ALU.add)
+
+        def tanh_term(i, c):
+            b, t = divmod(i, PACK)
+            if c.start == 0:
+                th[i] = ring.tile([P, S], F32, name="th")
+            nc.scalar.activation(th[i][:, c], bank[i, c.start][:], ACT.Tanh, bias=zero[:], scale=slope_t[:, b, t : t + 1])
+
+        def factors(i, c):
+            b, t = divmod(i, PACK)
+            gw[i] = turns[i]
+            nc.scalar.activation(gw[i][:, c], wgs_t[t][:, c], ACT.Copy, scale=gain_t[:, b, t : t + 1])
+
+        def cos_term(i, c):
+            if c.start == 0:
+                cs[i] = mag[i - 1] if i > 0 else keep.tile([P, S], F32, name="cs0")
+            nc.scalar.activation(cs[i][:, c], red[i][:, c], ACT.Sin, bias=half_pi[:], scale=-1.0)
+
+        def add_terms(eng, i, c):
+            eng.tensor_tensor(mag[i][:, c], th[i][:, c], cs[i][:, c], ALU.add)
+
+        def weigh(i, c):
+            nc.gpsimd.tensor_tensor(red[i][:, c], mag[i][:, c], gw[i][:, c], ALU.mult)
+
+        def put(i, c):
+            nc.vector.tensor_copy(page[i][:].indirect(entries(o2, c)), red[i][:, c])
+
+        planes = {}
+
+        def fetch(i, c):
+            b, t = divmod(i, PACK)
+            dst = planes[0][:, t, c] if b == 0 else planes[b, c.start][:, t, :]
+            nc.vector.tensor_copy(dst, page[i][:].indirect(entries(o3, c)))
+
+        xi, xa, xq, xm = {}, {}, {}, {}
+
+        def planes_of(b, c):
+            if b == 0:
+                src = planes[0][:, :, c]
+            else:
+                base = c.start // HALF * HALF
+                src = planes[b, base][:, :, c.start - base : c.stop - base]
+            return src.rearrange("p t (c i) -> p c t i", i=4)
+
+        def woven(tile):
+            return tile[:].rearrange("p (c i t) -> p c t i", i=4, t=PACK)
+
+        def weave(b, c):
+            xi[b, c.start] = ring.tile([P, PACK * (c.stop - c.start)], BF16, name="xi", align_bytes=64)
+            nc.scalar.copy(woven(xi[b, c.start]), planes_of(b, c))
+
+        def magnitude(b, c):
+            xa[b, c.start] = ring.tile([P, PACK * (c.stop - c.start)], BF16, name="xa", align_bytes=64)
+            nc.scalar.activation(woven(xa[b, c.start]), planes_of(b, c), ACT.Abs)
+
+        def quant_x(b, c):
+            xq[b, c.start] = quantize(xi[b, c.start][:], "xq%d_%d" % (b, c.start))
+
+        def quant_m(b, c):
+            xm[b, c.start] = quantize(xa[b, c.start][:], "xm%d_%d" % (b, c.start))
+
+        state = {}
+
+        def load_w2():
+            state["w2raw"] = []
+            for a in range(PASSES):
+                raw = ring.tile([P, PACK, N], F32, name="raw", align_bytes=64)
+                nc.sync.dma_start(raw[:], w2[a * KP : (a + 1) * KP, :].rearrange("(p i) n -> p i n", i=PACK))
+                state["w2raw"].append(raw)
+            state["w2b"] = ring.tile([P, PASSES * N * PACK], BF16, name="xi", align_bytes=64)
+
+        def load_w4():
+            w4w = keep.tile([P, PASSES, 2 * N], U8, name="w4w", align_bytes=64)
+            nc.sync.dma_start(w4w[:].bitcast(I32), w4_words.rearrange("a p n -> p a n").bitcast(I32))
+            for q in range(4):
+                nc.sync.dma_start(
+                    w4s[32 * q : 32 * q + 4, :, :].bitcast(I32),
+                    w4_scales[:, 4 * q : 4 * q + 4, :].rearrange("a r n -> r a n").bitcast(I32),
+                )
+            state["w4w"] = w4w
+
+        def cast_w2(a):
+            nc.scalar.copy(
+                state["w2b"][:, a * N * PACK : (a + 1) * N * PACK].rearrange("p (c i t) -> p c t i", i=4, t=PACK),
+                state["w2raw"][a][:].rearrange("p t (c i) -> p c t i", i=4),
+            )
+
+        def quant_w2():
+            w2c = keep.tile([P, PASSES * N], U32, name="w2c", align_bytes=64)
+            w2s = keep.tile([P, PASSES * N], U8, name="w2s", align_bytes=64)
+            for c0, c1 in ((0, 512), (512, PASSES * N)):
+                nc.vector.quantize_mx(
+                    out=w2c[:, c0:c1].bitcast(FP8X4), scales=w2s[:, c0:c1], in_=state["w2b"][:, PACK * c0 : PACK * c1]
+                )
+            state["w2c"], state["w2s"] = w2c, w2s
+
+        def load_out():
+            state["o4"] = load_list(offs4, "o4")
+            wgo_t = keep.tile([P, 1, S], F32, name="wgs0")
+            nc.sync.dma_start(wgo_t[:, 0, :], wgo)
+            state["wgo"] = wgo_t
+            state["page1"] = []
+            for nt in range(NT):
+                if nt < PASSES:
+                    pg = keep.tile([P, T2], F32, name="big%d" % nt, align_bytes=64)
+                else:
+                    pg = ring.tile([P, T2], F32, name="raw", align_bytes=64)
+                nc.sync.dma_start(pg[:], page1[nt * P : (nt + 1) * P, :])
+                state["page1"].append(pg)
+
+        banks = {}
+
+        def score(c, nt, b):
+            width = c.stop - c.start
+            if b == 0:
+                banks[c.start, nt] = psum.tile([P, width], F32, name="y")
+            y = banks[c.start, nt]
+            base = c.start // HALF * HALF if b == 0 else c.start
+            lo = c.start - base
+            c0 = b * N + nt * P
+            nc.tensor.matmul_mx(
+                out=y[:],
+                lhsT=state["w2c"][:, c0 : c0 + P].bitcast(FP8X4),
+                lhsT_scale=state["w2s"][:, c0 : c0 + P],
+                rhs=xq[b, base][0][:, lo : lo + width].bitcast(FP8X4),
+                rhs_scale=xq[b, base][1][:, lo : lo + width],
+                start=(b == 0),
+                stop=False,
+            )
+            step = width if width == HALF else P
+            for s0 in range(0, width, step):
+                nc.tensor.matmul_mx(
+                    out=y[:, s0 : s0 + step],
+                    lhsT=state["w4w"][:, b, 2 * nt * P : 2 * (nt + 1) * P].bitcast(FP4X4),
+                    lhsT_scale=w4s[:, b, nt * P : (nt + 1) * P],
+                    rhs=xm[b, base][0][:, lo + s0 : lo + s0 + step].bitcast(FP8X4),
+                    rhs_scale=xm[b, base][1][:, lo + s0 : lo + s0 + step],
+                    start=False,
+                    stop=(b == PASSES - 1 and s0 + step == width),
+                )
+
+        def finish(c, nt):
+            yt = ring.tile([P, c.stop - c.start], F32, name="mag", bufs=4)
+            nc.scalar.activation(yt[:], banks[c.start, nt][:], ACT.Tanh, bias=zero[:])
+            pg = state["page1"][nt]
+            nc.vector.tensor_tensor(pg[:].indirect(entries(state["o4"], c)), yt[:], state["wgo"][:, 0, c], ALU.mult)
+            if c.stop == S:
+                nc.sync.dma_start(out[nt * P : (nt + 1) * P, :], pg[:])
+
+        def side_work(j):
+            if j in (0, 1):
+                raws["b", j] = cast_w1(raws[1, j], False)
+                w1q[1, j] = quantize(raws["b", j][:], "w1q1%d" % j)
+            if j == 2:
+                load_w2()
+            if j in (2, 3):
+                cast_w2(j - 2)
+            if j == 4:
+                quant_w2()
+                load_w4()
+            if j == 5:
+                load_out()
+                weave(0, LOW)
+                quant_x(0, LOW)
+            if j == 6:
+                magnitude(0, LOW)
+                quant_m(0, LOW)
+            if j == 7:
+                weave(0, HIGH)
+                quant_x(0, HIGH)
+            if j == 8:
+                magnitude(0, HIGH)
+                quant_m(0, HIGH)
+
+        planes[0] = keep.tile([P, PACK, S], BF16, name="planes0")
+        planes[1, 0] = keep.tile([P, PACK, HALF], BF16, name="planes10")
+
+        def first_tile(c):
+            cos_term(0, c)
+            factors(0, c)
+            add_terms(nc.vector, 0, c)
+            nc.vector.tensor_tensor(page[0][:].indirect(entries(o2, c)), mag[0][:, c], gw[0][:, c], ALU.mult)
+
+        for c in (LOW, HIGH):
+            angle(0, c)
+            reduce_angle(0, c)
+            tanh_term(0, c)
+        first_tile(LOW)
+        for c in (LOW, HIGH):
+            angle(1, c)
+        reduce_angle(1, WHOLE)
+        first_tile(HIGH)
+        for c in (LOW, HIGH):
+            tanh_term(1, c)
+        side_work(0)
+        for j in range(1, TILES + 1):
+            if j + 1 < TILES:
+                load_page(j + 1)
+                angle(j + 1, LOW)
+                angle(j + 1, HIGH)
+            if j < TILES:
+                for c in (LOW, HIGH):
+                    cos_term(j, c)
+                    add_terms(nc.gpsimd, j, c)
+                factors(j, WHOLE)
+                weigh(j, WHOLE)
+            if j > 1:
+                put(j - 1, WHOLE)
+            if j + 1 < TILES:
+                tanh_term(j + 1, LOW)
+                tanh_term(j + 1, HIGH)
+            fetch(j - 1, WHOLE if j - 1 < PACK else LOW)
+            if j + 1 < TILES:
+                reduce_angle(j + 1, WHOLE)
+            side_work(j)
+        planes[1, HALF] = gw[TILES - 1][:].bitcast(BF16).rearrange("p (t c) -> p t c", t=PACK)
+        for nt in range(NT):
+            score(CHUNKS[0], nt, 0)
+        for i in range(PACK, TILES):
+            fetch(i, HIGH)
+        for n, c in enumerate(CHUNKS):
+            weave(1, c)
+            magnitude(1, c)
+            quant_x(1, c)
+            quant_m(1, c)
+            if n > 0:
+                for nt in range(NT):
+                    finish(CHUNKS[n - 1], nt)
+            for nt in range(NT):
+                if n > 0:
+                    score(c, nt, 0)
+                score(c, nt, 1)
+        for nt in range(NT):
+            finish(CHUNKS[-1], nt)

@@ -72,18 +72,18 @@ def tile_list_cabinet_repair_page_kernel(
 
         def load_w1(b, a):
             if (b, a) == (0, 0):
-                raw = keep.tile([P, PACK, KP], F32, name="wgs1")
+                raw = keep.tile([P, PACK, KP], F32, name="wgs0")
             else:
                 raw = ring.tile([P, PACK, KP], F32, name="raw", align_bytes=64)
             src = w1[a * KP : (a + 1) * KP, b * KP : (b + 1) * KP].rearrange("(p i) r -> p i r", i=PACK)
             nc.sync.dma_start(raw[:], src)
             return raw
 
-        def cast_w1(raw, on_vector):
-            if on_vector:
+        def cast_w1(raw, on_vector, tag="late_words"):
+            if on_vector and tag == "late_words":
                 wb = keep.tile([P, PACK * KP], BF16, name="late_words", align_bytes=64)
             else:
-                wb = ring.tile([P, PACK * KP], BF16, name="xa", align_bytes=64)
+                wb = ring.tile([P, PACK * KP], BF16, name="xa", align_bytes=64, bufs=3)
             dst = wb[:].rearrange("p (t m i) -> p m i t", t=PACK, i=PACK)
             src = raw[:].rearrange("p i (m t) -> p m i t", t=PACK)
             if on_vector:
@@ -127,7 +127,7 @@ def tile_list_cabinet_repair_page_kernel(
         nc.sync.dma_start(slope_t[:], slope.rearrange("(b p t) -> p b t", p=P, t=PACK))
         gain_t = keep.tile([P, PASSES, PACK], F32, name="gain_t")
         nc.sync.dma_start(gain_t[:], gain.rearrange("(b p t) -> p b t", p=P, t=PACK))
-        load_wgs(nc.sync, 0, [(0, 1)])
+        raws[1, 0] = load_w1(1, 0)
         o2 = load_list(offs2, "o2")
         load_page(0)
         o3 = load_list(offs3, "o3")
@@ -158,12 +158,15 @@ def tile_list_cabinet_repair_page_kernel(
         pick_words(0, HIGH)
         pick_scales(HIGH)
         pick_words(1, HIGH)
-        load_wgs(nc.gpsimd, 1, [(1, 2), (2, 4)])
-        raws[1, 0] = load_w1(1, 0)
+        load_wgs(nc.gpsimd, 0, [(0, 1), (1, 2), (2, 4)])
+        wb10 = cast_w1(raws[1, 0], True, "xa")
+        w1q[1, 0] = quantize(wb10[:], "w1q10")
         load_page(1)
         raws[1, 1] = load_w1(1, 1)
 
         mag, turns, th, gw, red, cs, bank = {}, {}, {}, {}, {}, {}, {}
+        ON_VECTOR, CAST_AT, W2_AT = 2, 2, 3
+        WEAVE_AT = 7
 
         def angle(i, c):
             b, t = divmod(i, PACK)
@@ -180,15 +183,22 @@ def tile_list_cabinet_repair_page_kernel(
                     stop=(a == PASSES - 1),
                 )
             if c.start == 0:
-                mag[i] = ring.tile([P, S], F32, name="mag", bufs=4)
+                mag[i] = ring.tile([P, S], F32, name="mag", bufs=3)
                 turns[i] = ring.tile([P, S], F32, name="turns", bufs=3, align_bytes=64)
                 red[i] = ring.tile([P, S], F32, name="red", bufs=3)
             nc.scalar.activation(mag[i][:, c], e[:], ACT.Abs)
             nc.scalar.activation(turns[i][:, c].bitcast(U32), mag[i][:, c], ACT.Copy, bias=-0.25, scale=1.0 / TWO_PI)
             bank[i, c.start] = e
+            if c.start == 0:
+                cs[i] = ring.tile([P, S], F32, name="cs", bufs=3)
+            if i >= ON_VECTOR:
+                nc.scalar.activation(cs[i][:, c], turns[i][:, c].bitcast(U32), ACT.Copy, scale=-TWO_PI)
 
         def reduce_angle(i, c):
-            nc.vector.scalar_tensor_tensor(red[i][:, c], turns[i][:, c].bitcast(I32), -TWO_PI, mag[i][:, c], ALU.mult, ALU.add)
+            if i < ON_VECTOR:
+                nc.vector.scalar_tensor_tensor(red[i][:, c], turns[i][:, c].bitcast(I32), -TWO_PI, mag[i][:, c], ALU.mult, ALU.add)
+            else:
+                nc.gpsimd.tensor_tensor(red[i][:, c], cs[i][:, c], mag[i][:, c], ALU.add)
 
         def tanh_term(i, c):
             b, t = divmod(i, PACK)
@@ -202,8 +212,6 @@ def tile_list_cabinet_repair_page_kernel(
             nc.scalar.activation(gw[i][:, c], wgs_t[t][:, c], ACT.Copy, scale=gain_t[:, b, t : t + 1])
 
         def cos_term(i, c):
-            if c.start == 0:
-                cs[i] = mag[i - 1] if i > 0 else keep.tile([P, S], F32, name="cs0")
             nc.scalar.activation(cs[i][:, c], red[i][:, c], ACT.Sin, bias=half_pi[:], scale=-1.0)
 
         def add_terms(eng, i, c):
@@ -236,11 +244,11 @@ def tile_list_cabinet_repair_page_kernel(
             return tile[:].rearrange("p (c i t) -> p c t i", i=4, t=PACK)
 
         def weave(b, c):
-            xi[b, c.start] = ring.tile([P, PACK * (c.stop - c.start)], BF16, name="xi", align_bytes=64)
+            xi[b, c.start] = ring.tile([P, PACK * (c.stop - c.start)], BF16, name="xi", align_bytes=64, bufs=3)
             nc.scalar.copy(woven(xi[b, c.start]), planes_of(b, c))
 
         def magnitude(b, c):
-            xa[b, c.start] = ring.tile([P, PACK * (c.stop - c.start)], BF16, name="xa", align_bytes=64)
+            xa[b, c.start] = ring.tile([P, PACK * (c.stop - c.start)], BF16, name="xa", align_bytes=64, bufs=3)
             nc.scalar.activation(woven(xa[b, c.start]), planes_of(b, c), ACT.Abs)
 
         def quant_x(b, c):
@@ -257,7 +265,7 @@ def tile_list_cabinet_repair_page_kernel(
                 raw = ring.tile([P, PACK, N], F32, name="raw", align_bytes=64)
                 nc.sync.dma_start(raw[:], w2[a * KP : (a + 1) * KP, :].rearrange("(p i) n -> p i n", i=PACK))
                 state["w2raw"].append(raw)
-            state["w2b"] = ring.tile([P, PASSES * N * PACK], BF16, name="xi", align_bytes=64)
+            state["w2b"] = ring.tile([P, PASSES * N * PACK], BF16, name="xi", align_bytes=64, bufs=3)
 
         def load_w4():
             w4w = keep.tile([P, PASSES, 2 * N], U8, name="w4w", align_bytes=64)
@@ -286,7 +294,7 @@ def tile_list_cabinet_repair_page_kernel(
 
         def load_out():
             state["o4"] = load_list(offs4, "o4")
-            wgo_t = keep.tile([P, 1, S], F32, name="wgs0")
+            wgo_t = keep.tile([P, 1, S], F32, name="late_words", align_bytes=64)
             nc.sync.dma_start(wgo_t[:, 0, :], wgo)
             state["wgo"] = wgo_t
             state["page1"] = []
@@ -330,7 +338,7 @@ def tile_list_cabinet_repair_page_kernel(
                 )
 
         def finish(c, nt):
-            yt = ring.tile([P, c.stop - c.start], F32, name="mag", bufs=4)
+            yt = ring.tile([P, c.stop - c.start], F32, name="mag", bufs=3)
             nc.scalar.activation(yt[:], banks[c.start, nt][:], ACT.Tanh, bias=zero[:])
             pg = state["page1"][nt]
             nc.vector.tensor_tensor(pg[:].indirect(entries(state["o4"], c)), yt[:], state["wgo"][:, 0, c], ALU.mult)
@@ -338,29 +346,24 @@ def tile_list_cabinet_repair_page_kernel(
                 nc.sync.dma_start(out[nt * P : (nt + 1) * P, :], pg[:])
 
         def side_work(j):
-            if j in (0, 1):
-                raws["b", j] = cast_w1(raws[1, j], False)
-                w1q[1, j] = quantize(raws["b", j][:], "w1q1%d" % j)
-            if j == 2:
+            if j == CAST_AT:
+                raws["b"] = cast_w1(raws[1, 1], False)
+                w1q[1, 1] = quantize(raws["b"][:], "w1q11")
+            if j == 3:
                 load_w2()
-            if j in (2, 3):
-                cast_w2(j - 2)
-            if j == 4:
-                quant_w2()
                 load_w4()
             if j == 5:
                 load_out()
-                weave(0, LOW)
-                quant_x(0, LOW)
-            if j == 6:
-                magnitude(0, LOW)
-                quant_m(0, LOW)
-            if j == 7:
-                weave(0, HIGH)
-                quant_x(0, HIGH)
-            if j == 8:
-                magnitude(0, HIGH)
-                quant_m(0, HIGH)
+            if j in (W2_AT, W2_AT + 1):
+                cast_w2(j - W2_AT)
+            if j == W2_AT + 1:
+                quant_w2()
+            for c in (LOW, HIGH):
+                if j == (WEAVE_AT if c == LOW else 7):
+                    weave(0, c)
+                    magnitude(0, c)
+                    quant_x(0, c)
+                    quant_m(0, c)
 
         planes[0] = keep.tile([P, PACK, S], BF16, name="planes0")
         planes[1, 0] = keep.tile([P, PACK, HALF], BF16, name="planes10")
@@ -382,26 +385,27 @@ def tile_list_cabinet_repair_page_kernel(
         first_tile(HIGH)
         for c in (LOW, HIGH):
             tanh_term(1, c)
-        side_work(0)
-        for j in range(1, TILES + 1):
-            if j + 1 < TILES:
-                load_page(j + 1)
-                angle(j + 1, LOW)
-                angle(j + 1, HIGH)
+        cos_term(1, WHOLE)
+        add_terms(nc.gpsimd, 1, WHOLE)
+        factors(1, WHOLE)
+        weigh(1, WHOLE)
+        fetch(0, WHOLE)
+        for j in range(2, TILES + 1):
             if j < TILES:
+                load_page(j)
                 for c in (LOW, HIGH):
-                    cos_term(j, c)
-                    add_terms(nc.gpsimd, j, c)
+                    angle(j, c)
+                    reduce_angle(j, c)
+                for c in (LOW, HIGH):
+                    tanh_term(j, c)
+                cos_term(j, LOW)
                 factors(j, WHOLE)
+                cos_term(j, HIGH)
+                for c in (LOW, HIGH):
+                    add_terms(nc.gpsimd, j, c)
                 weigh(j, WHOLE)
-            if j > 1:
-                put(j - 1, WHOLE)
-            if j + 1 < TILES:
-                tanh_term(j + 1, LOW)
-                tanh_term(j + 1, HIGH)
+            put(j - 1, WHOLE)
             fetch(j - 1, WHOLE if j - 1 < PACK else LOW)
-            if j + 1 < TILES:
-                reduce_angle(j + 1, WHOLE)
             side_work(j)
         planes[1, HALF] = gw[TILES - 1][:].bitcast(BF16).rearrange("p (t c) -> p t c", t=PACK)
         for nt in range(NT):

@@ -49,11 +49,7 @@ def tile_list_cabinet_repair_page_kernel(
             return lst[:, c.start // 16 : c.stop // 16]
 
         tab_sc = keep.tile([P, T], U8, name="tab_sc", align_bytes=64)
-        nc.gpsimd.memset(tab_sc[:].bitcast(I32), 0)
-        for q in range(4):
-            nc.gpsimd.dma_start(
-                tab_sc[32 * q : 32 * q + 8, :].bitcast(I32), tab_scales[:, 4 * q : 4 * q + 4, :].bitcast(I32)
-            )
+        nc.vector.memset(tab_sc[:].bitcast(I32), 0)
         ones = keep.tile([P, 1], F32, name="ones")
         nc.vector.memset(ones[:], 1.0)
         zero_in = keep.tile([P, 1], F32, name="zero_in")
@@ -72,7 +68,7 @@ def tile_list_cabinet_repair_page_kernel(
 
         def load_w1(b, a):
             if (b, a) == (0, 0):
-                raw = keep.tile([P, PACK, KP], F32, name="wgs0")
+                raw = pages.tile([P, PACK, KP], F32, name="page")
             else:
                 raw = ring.tile([P, PACK, KP], F32, name="raw", align_bytes=64)
             src = w1[a * KP : (a + 1) * KP, b * KP : (b + 1) * KP].rearrange("(p i) r -> p i r", i=PACK)
@@ -102,13 +98,10 @@ def tile_list_cabinet_repair_page_kernel(
         wgs_rows = wgs.rearrange("(q t) j -> q t j", t=PACK)
         wgs_t = {}
 
-        def load_wgs(queue, t0, groups):
-            w = keep.tile([P, groups[-1][1] - t0, S], F32, name="wgs%d" % t0)
-            for lo, hi in groups:
-                for q in range(4):
-                    queue.dma_start(w[32 * q : 32 * q + 32, lo - t0 : hi - t0, :], wgs_rows[:, lo:hi, :])
-                for t in range(lo, hi):
-                    wgs_t[t] = w[:, t - t0, :]
+        def load_wgs(t):
+            w = keep.tile([P, S], F32, name="wgs%d" % t)
+            nc.sync.dma_start(w[:], wgs_rows[:, t, :].unsqueeze(0).broadcast_to([4, 32, S]))
+            wgs_t[t] = w[:]
 
         page_rows = page0.rearrange("(b p t) m -> b t p m", p=P, t=PACK)
         page = {}
@@ -120,16 +113,29 @@ def tile_list_cabinet_repair_page_kernel(
         raws = {}
         o1 = load_list(offs, "o1")
         tab = [load_tab(0)]
+        for q in range(4):
+            nc.sync.dma_start(
+                tab_sc[32 * q : 32 * q + 8, :].bitcast(I32), tab_scales[:, 4 * q : 4 * q + 4, :].bitcast(I32)
+            )
         raws[0, 0] = load_w1(0, 0)
         tab.append(load_tab(1))
         raws[0, 1] = load_w1(0, 1)
         slope_t = keep.tile([P, PASSES, PACK], F32, name="slope_t")
-        nc.sync.dma_start(slope_t[:], slope.rearrange("(b p t) -> p b t", p=P, t=PACK))
+        nc.gpsimd.dma_start(slope_t[:], slope.rearrange("(b p t) -> p b t", p=P, t=PACK))
         gain_t = keep.tile([P, PASSES, PACK], F32, name="gain_t")
-        nc.sync.dma_start(gain_t[:], gain.rearrange("(b p t) -> p b t", p=P, t=PACK))
+        nc.gpsimd.dma_start(gain_t[:], gain.rearrange("(b p t) -> p b t", p=P, t=PACK))
         raws[1, 0] = load_w1(1, 0)
+        wgs_first = keep.tile([P, S], F32, name="wgs_first")
+        wgs_t[0] = wgs_first[:]
+
+        def load_first_wgs(c):
+            for q in range(4):
+                nc.sync.dma_start(wgs_first[32 * q : 32 * q + 32, c], wgs_rows[:, 0, c])
+
+        load_first_wgs(LOW)
         o2 = load_list(offs2, "o2")
         load_page(0)
+        load_first_wgs(HIGH)
         o3 = load_list(offs3, "o3")
 
         vw, vs = {}, {}
@@ -158,10 +164,11 @@ def tile_list_cabinet_repair_page_kernel(
         pick_words(0, HIGH)
         pick_scales(HIGH)
         pick_words(1, HIGH)
-        load_wgs(nc.gpsimd, 0, [(0, 1), (1, 2), (2, 4)])
+        load_wgs(1)
         wb10 = cast_w1(raws[1, 0], True, "xa")
         w1q[1, 0] = quantize(wb10[:], "w1q10")
         load_page(1)
+        load_wgs(2)
         raws[1, 1] = load_w1(1, 1)
 
         mag, turns, th, gw, red, cs, bank = {}, {}, {}, {}, {}, {}, {}
@@ -185,7 +192,7 @@ def tile_list_cabinet_repair_page_kernel(
             if c.start == 0:
                 mag[i] = ring.tile([P, S], F32, name="mag", bufs=3)
                 turns[i] = ring.tile([P, S], F32, name="turns", bufs=3, align_bytes=64)
-                red[i] = ring.tile([P, S], F32, name="red", bufs=3)
+                red[i] = ring.tile([P, S], F32, name="red", bufs=3, align_bytes=64)
             nc.scalar.activation(mag[i][:, c], e[:], ACT.Abs)
             nc.scalar.activation(turns[i][:, c].bitcast(U32), mag[i][:, c], ACT.Copy, bias=-0.25, scale=1.0 / TWO_PI)
             bank[i, c.start] = e
@@ -248,7 +255,10 @@ def tile_list_cabinet_repair_page_kernel(
             nc.scalar.copy(woven(xi[b, c.start]), planes_of(b, c))
 
         def magnitude(b, c):
-            xa[b, c.start] = ring.tile([P, PACK * (c.stop - c.start)], BF16, name="xa", align_bytes=64, bufs=3)
+            if (b, c.start) == (1, 0):
+                xa[b, c.start] = red[TILES - 1][:].bitcast(BF16)[:, S : 2 * S]
+            else:
+                xa[b, c.start] = ring.tile([P, PACK * (c.stop - c.start)], BF16, name="xa", align_bytes=64, bufs=3)
             nc.scalar.activation(woven(xa[b, c.start]), planes_of(b, c), ACT.Abs)
 
         def quant_x(b, c):
@@ -393,6 +403,8 @@ def tile_list_cabinet_repair_page_kernel(
         for j in range(2, TILES + 1):
             if j < TILES:
                 load_page(j)
+                if j == 2:
+                    load_wgs(3)
                 for c in (LOW, HIGH):
                     angle(j, c)
                     reduce_angle(j, c)
@@ -407,16 +419,19 @@ def tile_list_cabinet_repair_page_kernel(
             put(j - 1, WHOLE)
             fetch(j - 1, WHOLE if j - 1 < PACK else LOW)
             side_work(j)
-        planes[1, HALF] = gw[TILES - 1][:].bitcast(BF16).rearrange("p (t c) -> p t c", t=PACK)
+        planes[1, HALF] = red[TILES - 1][:].bitcast(BF16).rearrange("p (t c) -> p t c", t=PACK)
         for nt in range(NT):
             score(CHUNKS[0], nt, 0)
-        for i in range(PACK, TILES):
+        for i in range(PACK, PACK + 2):
             fetch(i, HIGH)
         for n, c in enumerate(CHUNKS):
             weave(1, c)
             magnitude(1, c)
             quant_x(1, c)
             quant_m(1, c)
+            if n == 0:
+                for i in range(PACK + 2, TILES):
+                    fetch(i, HIGH)
             if n > 0:
                 for nt in range(NT):
                     finish(CHUNKS[n - 1], nt)

@@ -76,8 +76,8 @@ def tile_list_cabinet_repair_page_kernel(
             return raw
 
         def cast_w1(raw, on_vector, tag="late_words"):
-            if on_vector and tag == "late_words":
-                wb = keep.tile([P, PACK * KP], BF16, name="late_words", align_bytes=64)
+            if tag != "xa":
+                wb = keep.tile([P, PACK * KP], BF16, name=tag, align_bytes=64)
             else:
                 wb = ring.tile([P, PACK * KP], BF16, name="xa", align_bytes=64, bufs=3)
             dst = wb[:].rearrange("p (t m i) -> p m i t", t=PACK, i=PACK)
@@ -88,10 +88,11 @@ def tile_list_cabinet_repair_page_kernel(
                 nc.scalar.copy(dst, src)
             return wb
 
-        def quantize(src, name):
+        def quantize(src, name, scales=None):
             width = src.shape[1] // PACK
             codes = keep.tile([P, width], U32, name=name + "_c", align_bytes=64)
-            scales = keep.tile([P, width], U8, name=name + "_s", align_bytes=64)
+            if scales is None:
+                scales = keep.tile([P, width], U8, name=name + "_s", align_bytes=64)
             nc.vector.quantize_mx(out=codes[:].bitcast(FP8X4), scales=scales[:], in_=src)
             return codes, scales
 
@@ -141,12 +142,8 @@ def tile_list_cabinet_repair_page_kernel(
         vw, vs = {}, {}
 
         def pick_words(a, c):
-            if c.start == 0:
-                vw[a, 0] = keep.tile([P, HALF], U32, name="vw%d" % a, align_bytes=64)
-            elif a == 0:
-                late = keep.tile([P, PASSES, HALF], U32, name="late_words", align_bytes=64)
-                for n in range(PASSES):
-                    vw[n, c.start] = late[:, n, :]
+            tag = "late_words" if (a, c) == (1, HIGH) else "vw%d_%d" % (a, c.start)
+            vw[a, c.start] = keep.tile([P, HALF], U32, name=tag, align_bytes=64)
             nc.vector.tensor_copy(vw[a, c.start][:], tab[a][:].bitcast(U32).indirect(entries(o1, c)))
 
         def pick_scales(c):
@@ -156,7 +153,7 @@ def tile_list_cabinet_repair_page_kernel(
         w1q = {}
         pick_words(0, LOW)
         pick_scales(LOW)
-        wb00 = cast_w1(raws[0, 0], False)
+        wb00 = cast_w1(raws[0, 0], False, "xa")
         pick_words(1, LOW)
         w1q[0, 0] = quantize(wb00[:], "w1q00")
         wb01 = cast_w1(raws[0, 1], True)
@@ -164,16 +161,17 @@ def tile_list_cabinet_repair_page_kernel(
         pick_words(0, HIGH)
         pick_scales(HIGH)
         pick_words(1, HIGH)
+        raws[1, 1] = load_w1(1, 1)
         load_wgs(1)
         wb10 = cast_w1(raws[1, 0], True, "xa")
         w1q[1, 0] = quantize(wb10[:], "w1q10")
         load_page(1)
         load_wgs(2)
-        raws[1, 1] = load_w1(1, 1)
 
         mag, turns, th, gw, red, cs, bank = {}, {}, {}, {}, {}, {}, {}
-        ON_VECTOR, CAST_AT, W2_AT = 2, 2, 3
-        WEAVE_AT = 7
+        AHEAD = False
+        SPLIT = 4
+        upper = {}
 
         def angle(i, c):
             b, t = divmod(i, PACK)
@@ -191,21 +189,26 @@ def tile_list_cabinet_repair_page_kernel(
                 )
             if c.start == 0:
                 mag[i] = ring.tile([P, S], F32, name="mag", bufs=3)
-                turns[i] = ring.tile([P, S], F32, name="turns", bufs=3, align_bytes=64)
-                red[i] = ring.tile([P, S], F32, name="red", bufs=3, align_bytes=64)
+                if i == 2:
+                    turns[i] = keep.tile([P, S], F32, name="odd", align_bytes=64)
+                else:
+                    turns[i] = ring.tile([P, S], F32, name="turns", bufs=4)
             nc.scalar.activation(mag[i][:, c], e[:], ACT.Abs)
             nc.scalar.activation(turns[i][:, c].bitcast(U32), mag[i][:, c], ACT.Copy, bias=-0.25, scale=1.0 / TWO_PI)
             bank[i, c.start] = e
-            if c.start == 0:
-                cs[i] = ring.tile([P, S], F32, name="cs", bufs=3)
-            if i >= ON_VECTOR:
-                nc.scalar.activation(cs[i][:, c], turns[i][:, c].bitcast(U32), ACT.Copy, scale=-TWO_PI)
+            if i >= SPLIT and c == HIGH:
+                back = ring.tile([P, HALF], F32, name="back", bufs=1)
+                nc.scalar.activation(back[:], turns[i][:, c].bitcast(U32), ACT.Copy, scale=-TWO_PI)
+                upper[i] = ring.tile([P, HALF], F32, name="upper")
+                nc.gpsimd.tensor_tensor(upper[i][:], back[:], mag[i][:, c], ALU.add)
 
         def reduce_angle(i, c):
-            if i < ON_VECTOR:
-                nc.vector.scalar_tensor_tensor(red[i][:, c], turns[i][:, c].bitcast(I32), -TWO_PI, mag[i][:, c], ALU.mult, ALU.add)
-            else:
-                nc.gpsimd.tensor_tensor(red[i][:, c], cs[i][:, c], mag[i][:, c], ALU.add)
+            if c.start == 0:
+                if i == 1:
+                    red[i] = ring.tile([P, S], F32, name="xi", align_bytes=64, bufs=3)
+                else:
+                    red[i] = keep.tile([P, S], F32, name=("even", "odd")[i % 2], align_bytes=64)
+            nc.vector.scalar_tensor_tensor(red[i][:, c], turns[i][:, c].bitcast(I32), -TWO_PI, mag[i][:, c], ALU.mult, ALU.add)
 
         def tanh_term(i, c):
             b, t = divmod(i, PACK)
@@ -215,17 +218,20 @@ def tile_list_cabinet_repair_page_kernel(
 
         def factors(i, c):
             b, t = divmod(i, PACK)
-            gw[i] = turns[i]
+            gw[i] = turns[i] if i != 2 else ring.tile([P, S], F32, name="turns", bufs=4)
             nc.scalar.activation(gw[i][:, c], wgs_t[t][:, c], ACT.Copy, scale=gain_t[:, b, t : t + 1])
 
         def cos_term(i, c):
-            nc.scalar.activation(cs[i][:, c], red[i][:, c], ACT.Sin, bias=half_pi[:], scale=-1.0)
+            if i not in cs:
+                cs[i] = ring.tile([P, S], F32, name="cs")
+            src = upper[i][:] if i >= SPLIT and c == HIGH else red[i][:, c]
+            nc.scalar.activation(cs[i][:, c], src, ACT.Sin, bias=half_pi[:], scale=-1.0)
 
         def add_terms(eng, i, c):
             eng.tensor_tensor(mag[i][:, c], th[i][:, c], cs[i][:, c], ALU.add)
 
-        def weigh(i, c):
-            nc.gpsimd.tensor_tensor(red[i][:, c], mag[i][:, c], gw[i][:, c], ALU.mult)
+        def weigh(eng, i):
+            eng.tensor_tensor(red[i][:], mag[i][:], gw[i][:], ALU.mult)
 
         def put(i, c):
             nc.vector.tensor_copy(page[i][:].indirect(entries(o2, c)), red[i][:, c])
@@ -262,10 +268,12 @@ def tile_list_cabinet_repair_page_kernel(
             nc.scalar.activation(woven(xa[b, c.start]), planes_of(b, c), ACT.Abs)
 
         def quant_x(b, c):
-            xq[b, c.start] = quantize(xi[b, c.start][:], "xq%d_%d" % (b, c.start))
+            plane = state["late"][:, c.start : c.stop] if b == 0 else None
+            xq[b, c.start] = quantize(xi[b, c.start][:], "xq%d_%d" % (b, c.start), plane)
 
         def quant_m(b, c):
-            xm[b, c.start] = quantize(xa[b, c.start][:], "xm%d_%d" % (b, c.start))
+            plane = state["late"][:, S + c.start : S + c.stop] if b == 0 else None
+            xm[b, c.start] = quantize(xa[b, c.start][:], "xm%d_%d" % (b, c.start), plane)
 
         state = {}
 
@@ -295,7 +303,7 @@ def tile_list_cabinet_repair_page_kernel(
 
         def quant_w2():
             w2c = keep.tile([P, PASSES * N], U32, name="w2c", align_bytes=64)
-            w2s = keep.tile([P, PASSES * N], U8, name="w2s", align_bytes=64)
+            w2s = state["late"][:, 2 * S : 2 * S + PASSES * N]
             for c0, c1 in ((0, 512), (512, PASSES * N)):
                 nc.vector.quantize_mx(
                     out=w2c[:, c0:c1].bitcast(FP8X4), scales=w2s[:, c0:c1], in_=state["w2b"][:, PACK * c0 : PACK * c1]
@@ -355,26 +363,6 @@ def tile_list_cabinet_repair_page_kernel(
             if c.stop == S:
                 nc.sync.dma_start(out[nt * P : (nt + 1) * P, :], pg[:])
 
-        def side_work(j):
-            if j == CAST_AT:
-                raws["b"] = cast_w1(raws[1, 1], False)
-                w1q[1, 1] = quantize(raws["b"][:], "w1q11")
-            if j == 3:
-                load_w2()
-                load_w4()
-            if j == 5:
-                load_out()
-            if j in (W2_AT, W2_AT + 1):
-                cast_w2(j - W2_AT)
-            if j == W2_AT + 1:
-                quant_w2()
-            for c in (LOW, HIGH):
-                if j == (WEAVE_AT if c == LOW else 7):
-                    weave(0, c)
-                    magnitude(0, c)
-                    quant_x(0, c)
-                    quant_m(0, c)
-
         planes[0] = keep.tile([P, PACK, S], BF16, name="planes0")
         planes[1, 0] = keep.tile([P, PACK, HALF], BF16, name="planes10")
 
@@ -396,29 +384,60 @@ def tile_list_cabinet_repair_page_kernel(
         for c in (LOW, HIGH):
             tanh_term(1, c)
         cos_term(1, WHOLE)
-        add_terms(nc.gpsimd, 1, WHOLE)
-        factors(1, WHOLE)
-        weigh(1, WHOLE)
         fetch(0, WHOLE)
+        load_page(2)
+        load_wgs(3)
+        for c in (LOW, HIGH):
+            angle(2, c)
+        factors(1, WHOLE)
+        add_terms(nc.vector, 1, WHOLE)
+        wb11 = cast_w1(raws[1, 1], False, "even")
+        w1q[1, 1] = quantize(wb11[:], "w1q11")
+        reduce_angle(2, WHOLE)
+        red[1] = keep.tile([P, S], F32, name="odd", align_bytes=64)
+        weigh(nc.vector, 1)
+        for c in (LOW, HIGH):
+            tanh_term(2, c)
+        load_page(3)
+        for c in (LOW, HIGH):
+            angle(3, c)
         for j in range(2, TILES + 1):
+            if j + 2 < TILES:
+                load_page(j + 2)
+            if j == 3:
+                load_w2()
+                load_w4()
+            if j == 5:
+                load_out()
             if j < TILES:
-                load_page(j)
-                if j == 2:
-                    load_wgs(3)
-                for c in (LOW, HIGH):
-                    angle(j, c)
-                    reduce_angle(j, c)
-                for c in (LOW, HIGH):
-                    tanh_term(j, c)
-                cos_term(j, LOW)
+                if AHEAD and j + 2 < TILES:
+                    for c in (LOW, HIGH):
+                        angle(j + 2, c)
+                cos_term(j, WHOLE if j < SPLIT else LOW)
                 factors(j, WHOLE)
-                cos_term(j, HIGH)
-                for c in (LOW, HIGH):
-                    add_terms(nc.gpsimd, j, c)
-                weigh(j, WHOLE)
+                add_terms(nc.gpsimd, j, WHOLE)
+                weigh(nc.gpsimd, j)
+                if not AHEAD and j + 2 < TILES:
+                    for c in (LOW, HIGH):
+                        angle(j + 2, c)
             put(j - 1, WHOLE)
+            if j + 1 < TILES:
+                reduce_angle(j + 1, WHOLE if j + 1 < SPLIT else LOW)
+                for c in (LOW, HIGH):
+                    tanh_term(j + 1, c)
+                if j + 1 >= SPLIT:
+                    cos_term(j + 1, HIGH)
             fetch(j - 1, WHOLE if j - 1 < PACK else LOW)
-            side_work(j)
+            if j == TILES - 1:
+                state["late"] = keep.tile([P, 3 * S], U8, name="even", align_bytes=64)
+                cast_w2(0)
+                cast_w2(1)
+                quant_w2()
+                for c in (LOW, HIGH):
+                    weave(0, c)
+                    magnitude(0, c)
+                    quant_x(0, c)
+                    quant_m(0, c)
         planes[1, HALF] = red[TILES - 1][:].bitcast(BF16).rearrange("p (t c) -> p t c", t=PACK)
         for nt in range(NT):
             score(CHUNKS[0], nt, 0)

import math
from contextlib import ExitStack

import concourse.mybir as mybir

K, T, S, H, N, T2 = 1024, 2048, 1024, 1024, 384, 2048
FLOPS = 2 * K * H * S + 4 * H * N * S

F32 = mybir.dt.float32
BF16 = mybir.dt.bfloat16
I32 = mybir.dt.int32
U32 = mybir.dt.uint32
U16 = mybir.dt.uint16
U8 = mybir.dt.uint8
FP8X4 = mybir.dt.float8_e4m3fn_x4
FP4X4 = mybir.dt.float4_e2m1fn_x4
ACT = mybir.ActivationFunctionType
ALU = mybir.AluOpType

P = 128
PACK = 4
KP = P * PACK
HALF = 512
PASSES = K // KP
TILES = H // P
NT = N // P
TWO_PI = 2.0 * math.pi
LOW, HIGH, WHOLE = slice(0, HALF), slice(HALF, S), slice(0, S)
CHUNKS = (slice(0, 256), slice(256, 512), slice(512, 1024))


def tile_list_cabinet_repair_page_kernel(
    tc, tab_words, tab_scales, offs, w1, slope, gain, wgs, page0, offs2, offs3, w2, w4_words, w4_scales, page1, wgo, offs4, out
):
    nc = tc.nc
    with ExitStack() as ctx:
        lists = ctx.enter_context(tc.tile_pool(name="lists", bufs=1))
        keep = ctx.enter_context(tc.tile_pool(name="keep", bufs=1))
        ring = ctx.enter_context(tc.tile_pool(name="ring", bufs=2))
        pages = ctx.enter_context(tc.tile_pool(name="pages", bufs=5))
        psum = ctx.enter_context(tc.psum_pool(name="psum", bufs=4))

        def load_list(src, name):
            t = lists.tile([P, S // 16], U16, name=name)
            nc.sync.dma_start(t[:], src)
            return t

        def entries(lst, c):
            return lst[:, c.start // 16 : c.stop // 16]

        tab_sc = keep.tile([P, T], U8, name="tab_sc", align_bytes=64)
        nc.vector.memset(tab_sc[:].bitcast(I32), 0)
        ones = keep.tile([P, 1], F32, name="ones")
        nc.vector.memset(ones[:], 1.0)
        zero_in = keep.tile([P, 1], F32, name="zero_in")
        nc.vector.memset(zero_in[:], 0.0)
        zero = keep.tile([P, 1], F32, name="zero")
        nc.scalar.activation(zero[:], zero_in[:], ACT.Silu)
        half_pi = keep.tile([P, 1], F32, name="half_pi")
        nc.vector.tensor_scalar(half_pi[:], ones[:], math.pi / 2, None, ALU.mult)
        w4s = keep.tile([P, PASSES, N], U8, name="w4s", align_bytes=64)
        nc.vector.memset(w4s[:].bitcast(I32), 0)

        def load_tab(a):
            t = keep.tile([P, T], I32, name="big%d" % a, align_bytes=64)
            nc.sync.dma_start(t[:], tab_words[a].rearrange("p t i -> p (t i)").bitcast(I32))
            return t

        def load_w1(b, a):
            if (b, a) == (0, 0):
                raw = pages.tile([P, PACK, KP], F32, name="page")
            else:
                raw = ring.tile([P, PACK, KP], F32, name="raw", align_bytes=64)
            src = w1[a * KP : (a + 1) * KP, b * KP : (b + 1) * KP].rearrange("(p i) r -> p i r", i=PACK)
            nc.sync.dma_start(raw[:], src)
            return raw

        def cast_w1(raw, on_vector, tag="late_words"):
            if tag != "xa":
                wb = keep.tile([P, PACK * KP], BF16, name=tag, align_bytes=64)
            else:
                wb = ring.tile([P, PACK * KP], BF16, name="xa", align_bytes=64, bufs=3)
            dst = wb[:].rearrange("p (t m i) -> p m i t", t=PACK, i=PACK)
            src = raw[:].rearrange("p i (m t) -> p m i t", t=PACK)
            if on_vector:
                nc.vector.tensor_copy(dst, src)
            else:
                nc.scalar.copy(dst, src)
            return wb

        def quantize(src, name, scales=None):
            width = src.shape[1] // PACK
            codes = keep.tile([P, width], U32, name=name + "_c", align_bytes=64)
            if scales is None:
                scales = keep.tile([P, width], U8, name=name + "_s", align_bytes=64)
            nc.vector.quantize_mx(out=codes[:].bitcast(FP8X4), scales=scales[:], in_=src)
            return codes, scales

        wgs_rows = wgs.rearrange("(q t) j -> q t j", t=PACK)
        wgs_t = {}

        def load_wgs(t):
            w = keep.tile([P, S], F32, name="wgs%d" % t)
            nc.sync.dma_start(w[:], wgs_rows[:, t, :].unsqueeze(0).broadcast_to([4, 32, S]))
            wgs_t[t] = w[:]

        page_rows = page0.rearrange("(b p t) m -> b t p m", p=P, t=PACK)
        page = {}

        def load_page(i):
            page[i] = pages.tile([P, T2], F32, name="page")
            nc.sync.dma_start(page[i][:], page_rows[i // PACK, i % PACK])

        raws = {}
        o1 = load_list(offs, "o1")
        tab = [load_tab(0)]
        for q in range(4):
            nc.sync.dma_start(
                tab_sc[32 * q : 32 * q + 8, :].bitcast(I32), tab_scales[:, 4 * q : 4 * q + 4, :].bitcast(I32)
            )
        raws[0, 0] = load_w1(0, 0)
        tab.append(load_tab(1))
        raws[0, 1] = load_w1(0, 1)
        slope_t = keep.tile([P, PASSES, PACK], F32, name="slope_t")
        nc.gpsimd.dma_start(slope_t[:], slope.rearrange("(b p t) -> p b t", p=P, t=PACK))
        gain_t = keep.tile([P, PASSES, PACK], F32, name="gain_t")
        nc.gpsimd.dma_start(gain_t[:], gain.rearrange("(b p t) -> p b t", p=P, t=PACK))
        raws[1, 0] = load_w1(1, 0)
        wgs_first = keep.tile([P, S], F32, name="wgs_first")
        wgs_t[0] = wgs_first[:]

        def load_first_wgs(c):
            for q in range(4):
                nc.sync.dma_start(wgs_first[32 * q : 32 * q + 32, c], wgs_rows[:, 0, c])

        load_first_wgs(LOW)
        o2 = load_list(offs2, "o2")
        load_page(0)
        load_first_wgs(HIGH)
        o3 = load_list(offs3, "o3")

        vw, vs = {}, {}

        def pick_words(a, c):
            tag = "late_words" if (a, c) == (1, HIGH) else "vw%d_%d" % (a, c.start)
            vw[a, c.start] = keep.tile([P, HALF], U32, name=tag, align_bytes=64)
            nc.vector.tensor_copy(vw[a, c.start][:], tab[a][:].bitcast(U32).indirect(entries(o1, c)))

        def pick_scales(c):
            vs[c.start] = keep.tile([P, HALF], U8, name="vs%d" % c.start, align_bytes=64)
            nc.vector.tensor_copy(vs[c.start][:], tab_sc[:].indirect(entries(o1, c)))

        w1q = {}
        pick_words(0, LOW)
        pick_scales(LOW)
        wb00 = cast_w1(raws[0, 0], False, "xa")
        pick_words(1, LOW)
        w1q[0, 0] = quantize(wb00[:], "w1q00")
        wb01 = cast_w1(raws[0, 1], True)
        w1q[0, 1] = quantize(wb01[:], "w1q01")
        pick_words(0, HIGH)
        pick_scales(HIGH)
        pick_words(1, HIGH)
        raws[1, 1] = load_w1(1, 1)
        load_wgs(1)
        wb10 = cast_w1(raws[1, 0], True, "xa")
        w1q[1, 0] = quantize(wb10[:], "w1q10")
        load_page(1)
        load_wgs(2)

        mag, turns, th, gw, red, cs, bank = {}, {}, {}, {}, {}, {}, {}
        AHEAD = False
        SPLIT = 4
        upper = {}

        def angle(i, c):
            b, t = divmod(i, PACK)
            e = psum.tile([P, HALF], F32, name="e")
            for a in range(PASSES):
                codes, scales = w1q[b, a]
                nc.tensor.matmul_mx(
                    out=e[:],
                    lhsT=codes[:, t * P : (t + 1) * P].bitcast(FP8X4),
                    lhsT_scale=scales[:, t * P : (t + 1) * P],
                    rhs=vw[a, c.start][:].bitcast(FP8X4),
                    rhs_scale=vs[c.start][4 * a : P, :],
                    start=(a == 0),
                    stop=(a == PASSES - 1),
                )
            if c.start == 0:
                mag[i] = ring.tile([P, S], F32, name="mag", bufs=3)
                if i == 2:
                    turns[i] = keep.tile([P, S], F32, name="odd", align_bytes=64)
                else:
                    turns[i] = ring.tile([P, S], F32, name="turns", bufs=4)
            nc.scalar.activation(mag[i][:, c], e[:], ACT.Abs)
            nc.scalar.activation(turns[i][:, c].bitcast(U32), mag[i][:, c], ACT.Copy, bias=-0.25, scale=1.0 / TWO_PI)
            bank[i, c.start] = e
            if i >= SPLIT and c == HIGH:
                back = ring.tile([P, HALF], F32, name="back", bufs=1)
                nc.scalar.activation(back[:], turns[i][:, c].bitcast(U32), ACT.Copy, scale=-TWO_PI)
                upper[i] = ring.tile([P, HALF], F32, name="upper")
                nc.gpsimd.tensor_tensor(upper[i][:], back[:], mag[i][:, c], ALU.add)

        def reduce_angle(i, c):
            if c.start == 0:
                if i == 1:
                    red[i] = ring.tile([P, S], F32, name="xi", align_bytes=64, bufs=3)
                else:
                    red[i] = keep.tile([P, S], F32, name=("even", "odd")[i % 2], align_bytes=64)
            nc.vector.scalar_tensor_tensor(red[i][:, c], turns[i][:, c].bitcast(I32), -TWO_PI, mag[i][:, c], ALU.mult, ALU.add)

        def tanh_term(i, c):
            b, t = divmod(i, PACK)
            if c.start == 0:
                th[i] = ring.tile([P, S], F32, name="th")
            nc.scalar.activation(th[i][:, c], bank[i, c.start][:], ACT.Tanh, bias=zero[:], scale=slope_t[:, b, t : t + 1])

        def factors(i, c):
            b, t = divmod(i, PACK)
            gw[i] = turns[i] if i != 2 else ring.tile([P, S], F32, name="turns", bufs=4)
            nc.scalar.activation(gw[i][:, c], wgs_t[t][:, c], ACT.Copy, scale=gain_t[:, b, t : t + 1])

        def cos_term(i, c):
            if i not in cs:
                cs[i] = ring.tile([P, S], F32, name="cs")
            src = upper[i][:] if i >= SPLIT and c == HIGH else red[i][:, c]
            nc.scalar.activation(cs[i][:, c], src, ACT.Sin, bias=half_pi[:], scale=-1.0)

        def add_terms(eng, i, c):
            eng.tensor_tensor(mag[i][:, c], th[i][:, c], cs[i][:, c], ALU.add)

        def weigh(eng, i):
            eng.tensor_tensor(red[i][:], mag[i][:], gw[i][:], ALU.mult)

        def put(i, c):
            nc.vector.tensor_copy(page[i][:].indirect(entries(o2, c)), red[i][:, c])

        planes = {}

        def fetch(i, c):
            b, t = divmod(i, PACK)
            dst = planes[0][:, t, c] if b == 0 else planes[b, c.start][:, t, :]
            nc.vector.tensor_copy(dst, page[i][:].indirect(entries(o3, c)))

        xi, xa, xq, xm = {}, {}, {}, {}

        def planes_of(b, c):
            if b == 0:
                src = planes[0][:, :, c]
            else:
                base = c.start // HALF * HALF
                src = planes[b, base][:, :, c.start - base : c.stop - base]
            return src.rearrange("p t (c i) -> p c t i", i=4)

        def woven(tile):
            return tile[:].rearrange("p (c i t) -> p c t i", i=4, t=PACK)

        def weave(b, c):
            xi[b, c.start] = ring.tile([P, PACK * (c.stop - c.start)], BF16, name="xi", align_bytes=64, bufs=3)
            nc.scalar.copy(woven(xi[b, c.start]), planes_of(b, c))

        def magnitude(b, c):
            if (b, c.start) == (1, 0):
                xa[b, c.start] = red[TILES - 1][:].bitcast(BF16)[:, S : 2 * S]
            else:
                xa[b, c.start] = ring.tile([P, PACK * (c.stop - c.start)], BF16, name="xa", align_bytes=64, bufs=3)
            nc.scalar.activation(woven(xa[b, c.start]), planes_of(b, c), ACT.Abs)

        def quant_x(b, c):
            plane = state["late"][:, c.start : c.stop] if b == 0 else None
            xq[b, c.start] = quantize(xi[b, c.start][:], "xq%d_%d" % (b, c.start), plane)

        def quant_m(b, c):
            plane = state["late"][:, S + c.start : S + c.stop] if b == 0 else None
            xm[b, c.start] = quantize(xa[b, c.start][:], "xm%d_%d" % (b, c.start), plane)

        state = {}

        def load_w2():
            state["w2raw"] = []
            for a in range(PASSES):
                raw = ring.tile([P, PACK, N], F32, name="raw", align_bytes=64)
                nc.sync.dma_start(raw[:], w2[a * KP : (a + 1) * KP, :].rearrange("(p i) n -> p i n", i=PACK))
                state["w2raw"].append(raw)
            state["w2b"] = ring.tile([P, PASSES * N * PACK], BF16, name="xi", align_bytes=64, bufs=3)

        def load_w4():
            w4w = keep.tile([P, PASSES, 2 * N], U8, name="w4w", align_bytes=64)
            nc.sync.dma_start(w4w[:].bitcast(I32), w4_words.rearrange("a p n -> p a n").bitcast(I32))
            for q in range(4):
                nc.sync.dma_start(
                    w4s[32 * q : 32 * q + 4, :, :].bitcast(I32),
                    w4_scales[:, 4 * q : 4 * q + 4, :].rearrange("a r n -> r a n").bitcast(I32),
                )
            state["w4w"] = w4w

        def cast_w2(a):
            nc.scalar.copy(
                state["w2b"][:, a * N * PACK : (a + 1) * N * PACK].rearrange("p (c i t) -> p c t i", i=4, t=PACK),
                state["w2raw"][a][:].rearrange("p t (c i) -> p c t i", i=4),
            )

        def quant_w2():
            w2c = keep.tile([P, PASSES * N], U32, name="w2c", align_bytes=64)
            w2s = state["late"][:, 2 * S : 2 * S + PASSES * N]
            for c0, c1 in ((0, 512), (512, PASSES * N)):
                nc.vector.quantize_mx(
                    out=w2c[:, c0:c1].bitcast(FP8X4), scales=w2s[:, c0:c1], in_=state["w2b"][:, PACK * c0 : PACK * c1]
                )
            state["w2c"], state["w2s"] = w2c, w2s

        def load_out():
            state["o4"] = load_list(offs4, "o4")
            wgo_t = keep.tile([P, 1, S], F32, name="late_words", align_bytes=64)
            nc.sync.dma_start(wgo_t[:, 0, :], wgo)
            state["wgo"] = wgo_t
            state["page1"] = []
            for nt in range(NT):
                if nt < PASSES:
                    pg = keep.tile([P, T2], F32, name="big%d" % nt, align_bytes=64)
                else:
                    pg = ring.tile([P, T2], F32, name="raw", align_bytes=64)
                nc.sync.dma_start(pg[:], page1[nt * P : (nt + 1) * P, :])
                state["page1"].append(pg)

        banks = {}

        def score(c, nt, b):
            width = c.stop - c.start
            if b == 0:
                banks[c.start, nt] = psum.tile([P, width], F32, name="y")
            y = banks[c.start, nt]
            base = c.start // HALF * HALF if b == 0 else c.start
            lo = c.start - base
            c0 = b * N + nt * P
            nc.tensor.matmul_mx(
                out=y[:],
                lhsT=state["w2c"][:, c0 : c0 + P].bitcast(FP8X4),
                lhsT_scale=state["w2s"][:, c0 : c0 + P],
                rhs=xq[b, base][0][:, lo : lo + width].bitcast(FP8X4),
                rhs_scale=xq[b, base][1][:, lo : lo + width],
                start=(b == 0),
                stop=False,
            )
            step = width if width == HALF else P
            for s0 in range(0, width, step):
                nc.tensor.matmul_mx(
                    out=y[:, s0 : s0 + step],
                    lhsT=state["w4w"][:, b, 2 * nt * P : 2 * (nt + 1) * P].bitcast(FP4X4),
                    lhsT_scale=w4s[:, b, nt * P : (nt + 1) * P],
                    rhs=xm[b, base][0][:, lo + s0 : lo + s0 + step].bitcast(FP8X4),
                    rhs_scale=xm[b, base][1][:, lo + s0 : lo + s0 + step],
                    start=False,
                    stop=(b == PASSES - 1 and s0 + step == width),
                )

        def finish(c, nt):
            yt = ring.tile([P, c.stop - c.start], F32, name="mag", bufs=3)
            nc.scalar.activation(yt[:], banks[c.start, nt][:], ACT.Tanh, bias=zero[:])
            pg = state["page1"][nt]
            nc.vector.tensor_tensor(pg[:].indirect(entries(state["o4"], c)), yt[:], state["wgo"][:, 0, c], ALU.mult)
            if c.stop == S:
                nc.sync.dma_start(out[nt * P : (nt + 1) * P, :], pg[:])

        planes[0] = keep.tile([P, PACK, S], BF16, name="planes0")
        planes[1, 0] = keep.tile([P, PACK, HALF], BF16, name="planes10")

        def first_tile(c):
            cos_term(0, c)
            factors(0, c)
            add_terms(nc.vector, 0, c)
            nc.vector.tensor_tensor(page[0][:].indirect(entries(o2, c)), mag[0][:, c], gw[0][:, c], ALU.mult)

        for c in (LOW, HIGH):
            angle(0, c)
            reduce_angle(0, c)
            tanh_term(0, c)
        first_tile(LOW)
        for c in (LOW, HIGH):
            angle(1, c)
        reduce_angle(1, WHOLE)
        first_tile(HIGH)
        for c in (LOW, HIGH):
            tanh_term(1, c)
        cos_term(1, WHOLE)
        fetch(0, WHOLE)
        load_page(2)
        load_wgs(3)
        for c in (LOW, HIGH):
            angle(2, c)
        factors(1, WHOLE)
        add_terms(nc.vector, 1, WHOLE)
        wb11 = cast_w1(raws[1, 1], False, "even")
        w1q[1, 1] = quantize(wb11[:], "w1q11")
        reduce_angle(2, WHOLE)
        red[1] = keep.tile([P, S], F32, name="odd", align_bytes=64)
        weigh(nc.vector, 1)
        for c in (LOW, HIGH):
            tanh_term(2, c)
        load_page(3)
        for c in (LOW, HIGH):
            angle(3, c)
        for j in range(2, TILES + 1):
            if j + 2 < TILES:
                load_page(j + 2)
            if j == 3:
                load_w2()
                load_w4()
            if j == 5:
                load_out()
            if j < TILES:
                if AHEAD and j + 2 < TILES:
                    for c in (LOW, HIGH):
                        angle(j + 2, c)
                cos_term(j, WHOLE if j < SPLIT else LOW)
                factors(j, WHOLE)
                add_terms(nc.gpsimd, j, WHOLE)
                weigh(nc.gpsimd, j)
                if not AHEAD and j + 2 < TILES:
                    for c in (LOW, HIGH):
                        angle(j + 2, c)
            put(j - 1, WHOLE)
            if j + 1 < TILES:
                reduce_angle(j + 1, WHOLE if j + 1 < SPLIT else LOW)
                for c in (LOW, HIGH):
                    tanh_term(j + 1, c)
                if j + 1 >= SPLIT:
                    cos_term(j + 1, HIGH)
            fetch(j - 1, WHOLE if j - 1 < PACK else LOW)
            if j == TILES - 1:
                state["late"] = keep.tile([P, 3 * S], U8, name="even", align_bytes=64)
                cast_w2(0)
                cast_w2(1)
                quant_w2()
                for c in (LOW, HIGH):
                    weave(0, c)
                    magnitude(0, c)
                    quant_x(0, c)
                    quant_m(0, c)
        planes[1, HALF] = red[TILES - 1][:].bitcast(BF16).rearrange("p (t c) -> p t c", t=PACK)
        for nt in range(NT):
            score(CHUNKS[0], nt, 0)
        for i in range(PACK, PACK + 2):
            fetch(i, HIGH)
        for n, c in enumerate(CHUNKS):
            weave(1, c)
            magnitude(1, c)
            quant_x(1, c)
            quant_m(1, c)
            if n == 0:
                for i in range(PACK + 2, TILES):
                    fetch(i, HIGH)
            if n > 0:
                for nt in range(NT):
                    finish(CHUNKS[n - 1], nt)
            for nt in range(NT):
                if n > 0:
                    score(c, nt, 0)
                score(c, nt, 1)
        for nt in range(NT):
            finish(CHUNKS[-1], nt)
